import numpy as np
import ml_dtypes


def mxq(x, axis, fmt="e4m3"):
    dtype, down = {"e4m3": (ml_dtypes.float8_e4m3fn, 7), "e5m2": (ml_dtypes.float8_e5m2, 14)}[fmt]
    v = np.moveaxis(np.asarray(x, np.float32).astype(ml_dtypes.bfloat16).astype(np.float64), axis, -1)
    blocks = v.reshape(v.shape[:-1] + (-1, 32))
    amax = np.abs(blocks).max(-1, keepdims=True)
    byte = np.maximum(np.where(amax > 0, np.frexp(amax)[1] - 1 + 127, 0) - down, 1)
    scale = np.exp2(byte - 127.0)
    codes = (blocks / scale).astype(np.float32).astype(dtype).astype(np.float64)
    return np.moveaxis((codes * scale).reshape(v.shape), -1, axis)


WIDE = False


def mx_kscale(k):
    if not WIDE:
        return np.ones(k)
    levels = np.array([10, -10, 5, -5, 0])
    if k % 512:
        return np.exp2(np.random.permutation(np.resize(levels, k // 32))).repeat(32)
    a = np.empty((k // 512, 16))
    for p in range(k // 512):
        a[p, :8] = np.random.permutation(np.resize(levels, 8))
        for g in range(8):
            far = levels[np.abs(levels - a[p, g]) >= 10]
            a[p, g + 8] = far[np.random.randint(len(far))]
    return np.exp2(a.ravel()).repeat(32)


def f64(x):
    return np.asarray(x).astype(np.float64)


def striped(idx):
    return np.tile(idx.reshape(-1, 16).T, (8, 1)).astype(np.uint16)


def unstriped(offs):
    return offs[:16].T.reshape(-1).astype(np.int64)


def striped8(idx):
    return np.concatenate([x.reshape(-1, 16).T for x in idx]).astype(np.uint16)


def runs(offs, k):
    lists = np.stack([offs[16 * r : 16 * r + 16].T.reshape(-1) for r in range(8)]).astype(np.int64)
    return lists[np.arange(k) % 512 // 64]


def pack_weight(w):
    k, n = w.shape
    w = f64(np.asarray(w, np.float32).astype(ml_dtypes.bfloat16)).reshape(k // 32, 32, n)
    amax = np.abs(w).max(1)
    byte = np.clip(np.where(amax > 0, np.frexp(amax)[1] - 1 + 127 - 7, 1), 1, 254)
    scaled = (w * np.exp2(127.0 - byte)[:, None, :]).reshape(k, n).astype(np.float32)
    words = np.ascontiguousarray(scaled.reshape(k // 512, 128, 4, n).transpose(0, 1, 3, 2)).astype(ml_dtypes.float8_e4m3fn).view(np.uint8)
    return words, np.ascontiguousarray(byte.astype(np.uint8).reshape(k // 512, 16, n))


def unpack_weight(words, scales):
    g, p, n, _ = words.shape
    vals = np.ascontiguousarray(words).view(ml_dtypes.float8_e4m3fn).astype(np.float64) * np.repeat(np.exp2(scales.astype(np.float64) - 127.0), 8, axis=1)[..., None]
    return vals.transpose(0, 1, 3, 2).reshape(g * 512, n)


E2M1 = np.array([0.0, 0.5, 1.0, 1.5, 2.0, 3.0, 4.0, 6.0, -0.0, -0.5, -1.0, -1.5, -2.0, -3.0, -4.0, -6.0])


def pack_fp4(w):
    k, n = w.shape
    w = f64(np.asarray(w, np.float32).astype(ml_dtypes.bfloat16)).reshape(k // 32, 32, n)
    amax = np.abs(w).max(1)
    mant, ex = np.frexp(amax / 6.0)
    byte = np.clip(np.where(amax > 0, np.where(mant > 0.5, ex, ex - 1) + 127, 1), 1, 254)
    scaled = (w * np.exp2(127.0 - byte)[:, None, :]).reshape(k, n).astype(np.float32)
    c = np.ascontiguousarray(scaled.reshape(k // 512, 128, 4, n).transpose(0, 1, 3, 2)).astype(ml_dtypes.float4_e2m1fn).view(np.uint8) & 0xF
    words = (c[..., 0::2] | (c[..., 1::2] << 4)).reshape(k // 512, 128, 2 * n)
    return np.ascontiguousarray(words), np.ascontiguousarray(byte.astype(np.uint8).reshape(k // 512, 16, n))


def unpack_fp4(words, scales):
    g, _, n = scales.shape
    words = np.ascontiguousarray(words).reshape(g, 128, n, 2)
    nib = np.empty((g, 128, n, 4), np.uint8)
    nib[..., 0::2] = words & 0xF
    nib[..., 1::2] = words >> 4
    vals = E2M1[nib] * np.repeat(np.exp2(scales.astype(np.float64) - 127.0), 8, axis=1)[..., None]
    return vals.transpose(0, 1, 3, 2).reshape(g * 512, n)


def sigmoid(v):
    return 1.0 / (1.0 + np.exp(-np.maximum(v, -700.0)))

def planes(y):
    n, m = y.shape
    v = y.astype(np.float32).astype(ml_dtypes.bfloat16).astype(np.float64).reshape(n // 32, 32, m)
    top = np.abs(v).max(1)
    byte = np.clip(np.where(top > 0, np.frexp(top)[1] - 1 + 127 - 7, 1), 1, 254)
    codes = (v * np.exp2(127.0 - byte)[:, None, :]).reshape(n, m).astype(np.float32).astype(ml_dtypes.float8_e4m3fn).view(np.uint8)
    words = codes.reshape(n // 512, 128, 4, m).transpose(0, 1, 3, 2)
    return np.ascontiguousarray(words), np.ascontiguousarray(byte.astype(np.uint8).reshape(n // 512, 16, m))


K, T, S, N, G, H = 512, 2048, 512, 512, 2048, 512


def setup_inputs():
    n = np.random.standard_normal
    s = mx_kscale(K)[:, None]
    u = mx_kscale(S)
    packed_xT = pack_weight(n((K, T)) * s)
    packed_dT = pack_weight(n((K, G)) / s)
    packed_w1 = pack_fp4(n((H, N)) / np.sqrt(H) / u[:, None])
    return {
        "x_words": packed_xT[0],
        "x_scales": packed_xT[1],
        "d_words": packed_dT[0],
        "d_scales": packed_dT[1],
        "gn": (np.random.uniform(0.5, 1.5, (H, 1)) * u[:, None]).astype(np.float32),
        "w1_words": packed_w1[0],
        "w1_scales": packed_w1[1],
        "offs": striped(np.random.permutation(T)[:S]),
        "k1": striped8(np.random.randint(0, G, (8, H))),
        "two": striped(np.random.permutation(T)[:S]),
        "n1": striped8(np.stack([np.random.permutation(S) for _ in range(8)])),
        "n2": striped8(np.stack([np.random.permutation(S) for _ in range(8)])),
        "n3": striped8(np.stack([np.random.permutation(S) for _ in range(8)])),
        "n4": striped8(np.stack([np.random.permutation(S) for _ in range(8)])),
        "n5": striped8(np.stack([np.random.permutation(S) for _ in range(8)])),
    }


def reference(x_words, x_scales, d_words, d_scales, gn, w1_words, w1_scales, offs, k1, two, n1, n2, n3, n4, n5):
    d_k1 = unpack_weight(d_words, d_scales)[np.arange(K)[:, None], runs(k1, K)]
    xq = unpack_weight(x_words, x_scales)[:, unstriped(offs)]
    a = 0.0625 * (d_k1.T @ xq)
    x_two = unpack_weight(x_words, x_scales)[:, unstriped(two)]
    b = 0.0625 * (d_k1.T @ x_two)
    z = f64(gn) * (a[np.arange(H)[:, None], runs(n1, H)] - (np.tanh(b) * (b[np.arange(H)[:, None], runs(n2, H)])))
    h = unpack_fp4(w1_words, w1_scales).T @ mxq(z, 0, "e4m3")
    out_0 = (h[np.arange(N)[:, None], runs(n3, N)]) * sigmoid(h) + (h[np.arange(N)[:, None], runs(n4, N)]) * (sigmoid(h[np.arange(N)[:, None], runs(n5, N)]))
    return (out_0,) + planes(out_0)

@@ -1,0 +1,195 @@
+import concourse.mybir as mybir
+
+F32 = mybir.dt.float32
+BF16 = mybir.dt.bfloat16
+I32 = mybir.dt.int32
+U32 = mybir.dt.uint32
+U16 = mybir.dt.uint16
+U8 = mybir.dt.uint8
+FP8X4 = mybir.dt.float8_e4m3fn_x4
+FP4X4 = mybir.dt.float4_e2m1fn_x4
+ALU = mybir.AluOpType
+ACT = mybir.ActivationFunctionType
+
+P = 128
+PACK = 4
+TABLE = 2048
+S = 512
+FLOPS = 3 * 2 * 512 * 512 * 512
+Z_PIECES = ((0, 256), (256, 512))
+O_PIECES = ((0, 256), (256, 512))
+
+
+def tile_picked_twkssoftbwsum_none_po_kernel(
+    tc, x_words, x_scales, d_words, d_scales, gn, w1_words, w1_scales,
+    offs, k1, two, n1, n2, n3, n4, n5, out_0, out_1, out_2,
+):
+    nc = tc.nc
+    with tc.tile_pool(name="keep", bufs=1) as keep, tc.psum_pool(name="psum", bufs=1) as psum:
+
+        def sb(name, shape, dtype):
+            return keep.tile(shape, dtype, name=name, align_bytes=64)
+
+        def load_list(name, src):
+            t = sb(name, [P, S // 16], U16)
+            nc.sync.dma_start(t[:], src)
+            return t
+
+        def entries(lst, lo, hi):
+            return lst[:, lo // 16 : hi // 16]
+
+        def woven(ap):
+            return ap.rearrange("p (c i t) -> p c t i", i=4, t=PACK)
+
+        def planes4(ap):
+            return ap.rearrange("p t (c i) -> p c t i", i=4)
+
+        d_sc = sb("d_sc", [P, TABLE], U8)
+        x_sc = sb("x_sc", [P, TABLE], U8)
+        w_sc = sb("w_sc", [P, S], U8)
+        nc.vector.memset(d_sc[:].bitcast(I32), 0)
+        nc.vector.memset(x_sc[:].bitcast(I32), 0)
+        nc.vector.memset(w_sc[:].bitcast(I32), 0)
+
+        k1_t = load_list("k1_t", k1)
+        for e in range(2):
+            nc.scalar.dma_start(d_sc[e:P:16, :].bitcast(I32), d_scales[0].bitcast(I32)[e:16:2, :])
+        two_t = load_list("two_t", two)
+        offs_t = load_list("offs_t", offs)
+        d_w = sb("d_w", [P, TABLE], U32)
+        x_w = sb("x_w", [P, TABLE], U32)
+        nc.sync.dma_start(d_w[:].bitcast(I32), d_words[0].rearrange("p n r -> p (n r)").bitcast(I32))
+        nc.sync.dma_start(x_w[:].bitcast(I32), x_words[0].rearrange("p n r -> p (n r)").bitcast(I32))
+        for q in range(4):
+            nc.scalar.dma_start(x_sc[32 * q : 32 * q + 4, :].bitcast(I32), x_scales[0].bitcast(I32)[4 * q : 4 * q + 4, :])
+
+        key_sc_raw = sb("key_sc_raw", [P, S], U8)
+        key_sc = sb("key_sc", [P, S], U8)
+        nc.vector.tensor_copy(key_sc_raw[:], d_sc[:].indirect(k1_t[:]))
+        nc.vector.tensor_copy(key_sc[:].rearrange("p (t m) -> p m t", t=PACK), key_sc_raw[:].rearrange("p (m t) -> p m t", t=PACK))
+        for e in range(2):
+            nc.scalar.dma_start(key_sc[2 + e : P : 32, :].bitcast(I32), key_sc[16 + e : P : 32, :].bitcast(I32))
+
+        gn_t = sb("gn_t", [P, PACK], F32)
+        nc.sync.dma_start(gn_t[:], gn.rearrange("(p t) o -> p (t o)", t=PACK))
+        n2_t = load_list("n2_t", n2)
+        n1_t = load_list("n1_t", n1)
+        w_w = sb("w_w", [P, 2 * S], U8)
+        nc.sync.dma_start(w_w[:].bitcast(I32), w1_words[0].bitcast(I32))
+        for q in range(4):
+            nc.sync.dma_start(w_sc[32 * q : 32 * q + 4, :].bitcast(I32), w1_scales[0].bitcast(I32)[4 * q : 4 * q + 4, :])
+        n3_t = load_list("n3_t", n3)
+        n5_t = load_list("n5_t", n5)
+        n4_t = load_list("n4_t", n4)
+
+        gain = sb("gain", [P, PACK], F32)
+        nc.gpsimd.tensor_scalar(gain[:], gn_t[:], 0.0625, 0.0, ALU.mult, ALU.add)
+
+        two_sc = sb("two_sc", [P, S], U8)
+        nc.vector.tensor_copy(two_sc[:], x_sc[:].indirect(two_t[:]))
+        key_raw = sb("key_raw", [P, S], U32)
+        key_w = sb("key_w", [P, S], U32)
+        nc.vector.tensor_copy(key_raw[:], d_w[:].indirect(k1_t[:]))
+        nc.vector.tensor_copy(
+            key_w[:].bitcast(I32).rearrange("p (t m) -> p m t", t=PACK),
+            key_raw[:].bitcast(I32).rearrange("p (m t) -> p m t", t=PACK),
+        )
+        two_w = sb("two_w", [P, S], U32)
+        nc.vector.tensor_copy(two_w[:], x_w[:].indirect(two_t[:]))
+
+        def scores(t, words, scales, tag):
+            acc = psum.tile([P, S], F32, name=tag)
+            cols = slice(t * P, (t + 1) * P)
+            nc.tensor.matmul_mx(
+                acc[:], lhsT=key_w[:, cols].bitcast(FP8X4), lhsT_scale=key_sc[:, cols],
+                rhs=words[:].bitcast(FP8X4), rhs_scale=scales[:], start=True, stop=True,
+            )
+            return acc
+
+        b_win, tanh_b = [], []
+        for t in range(PACK):
+            acc = scores(t, two_w, two_sc, f"bank{t}")
+            b_win.append(sb(f"b_win{t}", [P, S], F32))
+            tanh_b.append(sb(f"tanh_b{t}", [P, S], F32))
+            nc.scalar.activation(b_win[t][:], acc[:], ACT.Copy, scale=gain[:, t : t + 1])
+            nc.scalar.activation(tanh_b[t][:], acc[:], ACT.Tanh, scale=0.0625)
+
+        idx_sc = sb("idx_sc", [P, S], U8)
+        idx_w = sb("idx_w", [P, S], U32)
+        nc.vector.tensor_copy(idx_sc[:], x_sc[:].indirect(offs_t[:]))
+        nc.vector.tensor_copy(idx_w[:], x_w[:].indirect(offs_t[:]))
+
+        w_deal = sb("w_deal", [P, 2 * S], U8)
+        w_sc_deal = sb("w_sc_deal", [P, S], U8)
+        nc.vector.tensor_copy(
+            w_deal[:].rearrange("p (t m b) -> p m t b", t=PACK, b=2), w_w[:].rearrange("p (m t b) -> p m t b", t=PACK, b=2)
+        )
+        nc.vector.tensor_copy(w_sc_deal[:].rearrange("p (t m) -> p m t", t=PACK), w_sc[:].rearrange("p (m t) -> p m t", t=PACK))
+
+        a_win = []
+        for t in range(PACK):
+            acc = scores(t, idx_w, idx_sc, f"bank{PACK + t}")
+            a_win.append(sb(f"a_win{t}", [P, S], F32))
+            if t == 0:
+                nc.scalar.activation(a_win[t][:], acc[:], ACT.Copy, scale=gain[:, t : t + 1])
+            else:
+                nc.vector.tensor_scalar(a_win[t][:], acc[:], gain[:, t : t + 1], None, ALU.mult)
+
+        z_codes = sb("z_codes", [P, S], U32)
+        z_sc = sb("z_sc", [P, S], U8)
+        h_acc = [psum.tile([P, S], F32, name=f"bank{t}") for t in range(PACK)]
+        for lo, hi in Z_PIECES:
+            n = hi - lo
+            a_pick = sb(f"a_pick{lo}", [P, PACK, n], F32)
+            b_prod = sb(f"b_prod{lo}", [P, PACK, n], F32)
+            for t in range(PACK):
+                nc.vector.tensor_tensor(b_prod[:, t, :], b_win[t][:].indirect(entries(n2_t, lo, hi)), tanh_b[t][:, lo:hi], ALU.mult)
+                nc.scalar.activation(a_pick[:, t, :], a_win[t][:].indirect(entries(n1_t, lo, hi)), ACT.Copy)
+            z_bf = sb(f"z_bf{lo}", [P, PACK * n], BF16)
+            nc.vector.tensor_tensor(woven(z_bf[:]), planes4(a_pick[:]), planes4(b_prod[:]), ALU.subtract)
+            nc.vector.quantize_mx(z_codes[:, lo:hi].bitcast(FP8X4), z_sc[:, lo:hi], z_bf[:])
+            for t in range(PACK):
+                nc.tensor.matmul_mx(
+                    h_acc[t][:, lo:hi], lhsT=w_deal[:, 2 * t * P : 2 * (t + 1) * P].bitcast(FP4X4),
+                    lhsT_scale=w_sc_deal[:, t * P : (t + 1) * P],
+                    rhs=z_codes[:, lo:hi].bitcast(FP8X4), rhs_scale=z_sc[:, lo:hi], start=True, stop=True,
+                )
+
+        h_win, sig_h = [], []
+        for t in range(PACK):
+            h_win.append(sb(f"h_win{t}", [P, S], F32))
+            sig_h.append(sb(f"sig_h{t}", [P, S], F32))
+            if t % 2 == 0:
+                nc.vector.tensor_copy(h_win[t][:], h_acc[t][:])
+            else:
+                nc.scalar.activation(h_win[t][:], h_acc[t][:], ACT.Copy)
+
+        o_codes = sb("o_codes", [P, S], U32)
+        o_sc = sb("o_sc", [P, S], U8)
+        out_rows = out_0.rearrange("(p t) j -> p t j", t=PACK)
+        out_words = out_1[0].rearrange("p n r -> p (n r)").bitcast(I32)
+        for lo, hi in O_PIECES:
+            n = hi - lo
+            gate = sb(f"gate{lo}", [P, PACK, n], F32)
+            first = sb(f"first{lo}", [P, PACK, n], F32)
+            second = sb(f"second{lo}", [P, PACK, n], F32)
+            res = sb(f"res{lo}", [P, PACK, n], F32)
+            for t in range(PACK):
+                if lo == 0:
+                    nc.scalar.activation(sig_h[t][:], h_win[t][:], ACT.Sigmoid)
+                nc.scalar.activation(gate[:, t, :], h_win[t][:].indirect(entries(n5_t, lo, hi)), ACT.Sigmoid)
+                nc.vector.tensor_tensor(first[:, t, :], h_win[t][:].indirect(entries(n3_t, lo, hi)), sig_h[t][:, lo:hi], ALU.mult)
+                nc.vector.tensor_tensor(second[:, t, :], h_win[t][:].indirect(entries(n4_t, lo, hi)), gate[:, t, :], ALU.mult)
+                if t % 2 == 1:
+                    nc.vector.tensor_tensor(res[:, t - 1 : t + 1, :], first[:, t - 1 : t + 1, :], second[:, t - 1 : t + 1, :], ALU.add)
+            nc.sync.dma_start(out_rows[:, :, lo:hi], res[:])
+            o_bf = sb(f"o_bf{lo}", [P, PACK * n], BF16)
+            if hi < S:
+                nc.scalar.copy(woven(o_bf[:]), planes4(res[:]))
+            else:
+                nc.vector.tensor_copy(woven(o_bf[:]), planes4(res[:]))
+            nc.vector.quantize_mx(o_codes[:, lo:hi].bitcast(FP8X4), o_sc[:, lo:hi], o_bf[:])
+            nc.sync.dma_start(out_words[:, lo:hi], o_codes[:, lo:hi].bitcast(I32))
+        for q in range(4):
+            eng = nc.sync if q % 2 else nc.scalar
+            eng.dma_start(out_2[0].bitcast(I32)[4 * q : 4 * q + 4, :], o_sc[32 * q : 32 * q + 4, :].bitcast(I32))

@@ -16,8 +16,8 @@ PACK = 4
 TABLE = 2048
 S = 512
 FLOPS = 3 * 2 * 512 * 512 * 512
-Z_PIECES = ((0, 256), (256, 512))
-O_PIECES = ((0, 256), (256, 512))
+Z_PIECES = ((0, 256), (256, 384), (384, 512))
+O_PIECES = ((0, 256), (256, 384), (384, 512))
 
 
 def tile_picked_twkssoftbwsum_none_po_kernel(
@@ -47,48 +47,54 @@ def tile_picked_twkssoftbwsum_none_po_kernel(
         d_sc = sb("d_sc", [P, TABLE], U8)
         x_sc = sb("x_sc", [P, TABLE], U8)
         w_sc = sb("w_sc", [P, S], U8)
-        nc.vector.memset(d_sc[:].bitcast(I32), 0)
-        nc.vector.memset(x_sc[:].bitcast(I32), 0)
-        nc.vector.memset(w_sc[:].bitcast(I32), 0)
+        warm = sb("warm", [P, 1], F32)
+        nc.vector.memset(warm[:], 0.0)
+        warm_out = sb("warm_out", [P, 1], F32)
+        nc.scalar.activation(warm_out[:], warm[:], ACT.Sigmoid)
 
+        nc.vector.memset(x_sc[:].bitcast(I32), 0)
         k1_t = load_list("k1_t", k1)
-        for e in range(2):
-            nc.scalar.dma_start(d_sc[e:P:16, :].bitcast(I32), d_scales[0].bitcast(I32)[e:16:2, :])
+        nc.sync.dma_start(d_sc[:].bitcast(I32), d_scales[0].bitcast(I32).unsqueeze(1).to_broadcast([16, 8, TABLE // 4]))
         two_t = load_list("two_t", two)
-        offs_t = load_list("offs_t", offs)
+        for q in range(4):
+            nc.sync.dma_start(x_sc[32 * q : 32 * q + 4, :].bitcast(I32), x_scales[0].bitcast(I32)[4 * q : 4 * q + 4, :])
         d_w = sb("d_w", [P, TABLE], U32)
         x_w = sb("x_w", [P, TABLE], U32)
         nc.sync.dma_start(d_w[:].bitcast(I32), d_words[0].rearrange("p n r -> p (n r)").bitcast(I32))
-        nc.sync.dma_start(x_w[:].bitcast(I32), x_words[0].rearrange("p n r -> p (n r)").bitcast(I32))
-        for q in range(4):
-            nc.scalar.dma_start(x_sc[32 * q : 32 * q + 4, :].bitcast(I32), x_scales[0].bitcast(I32)[4 * q : 4 * q + 4, :])
-
-        key_sc_raw = sb("key_sc_raw", [P, S], U8)
-        key_sc = sb("key_sc", [P, S], U8)
-        nc.vector.tensor_copy(key_sc_raw[:], d_sc[:].indirect(k1_t[:]))
-        nc.vector.tensor_copy(key_sc[:].rearrange("p (t m) -> p m t", t=PACK), key_sc_raw[:].rearrange("p (m t) -> p m t", t=PACK))
-        for e in range(2):
-            nc.scalar.dma_start(key_sc[2 + e : P : 32, :].bitcast(I32), key_sc[16 + e : P : 32, :].bitcast(I32))
-
-        gn_t = sb("gn_t", [P, PACK], F32)
-        nc.sync.dma_start(gn_t[:], gn.rearrange("(p t) o -> p (t o)", t=PACK))
         n2_t = load_list("n2_t", n2)
         n1_t = load_list("n1_t", n1)
-        w_w = sb("w_w", [P, 2 * S], U8)
-        nc.sync.dma_start(w_w[:].bitcast(I32), w1_words[0].bitcast(I32))
-        for q in range(4):
-            nc.sync.dma_start(w_sc[32 * q : 32 * q + 4, :].bitcast(I32), w1_scales[0].bitcast(I32)[4 * q : 4 * q + 4, :])
+        nc.sync.dma_start(x_w[:].bitcast(I32), x_words[0].rearrange("p n r -> p (n r)").bitcast(I32))
+        offs_t = load_list("offs_t", offs)
         n3_t = load_list("n3_t", n3)
         n5_t = load_list("n5_t", n5)
         n4_t = load_list("n4_t", n4)
 
+        w_w = sb("w_w", [P, 2 * S], U8)
+        nc.gpsimd.dma_start(w_w[:].bitcast(I32), w1_words[0].bitcast(I32))
+        gn_t = sb("gn_t", [P, PACK], F32)
+        nc.gpsimd.dma_start(gn_t[:], gn.rearrange("(p t) o -> p (t o)", t=PACK))
+        nc.gpsimd.memset(w_sc[:].bitcast(I32), 0)
+        for q in range(4):
+            nc.gpsimd.dma_start(w_sc[32 * q : 32 * q + 4, :].bitcast(I32), w1_scales[0].bitcast(I32)[4 * q : 4 * q + 4, :])
         gain = sb("gain", [P, PACK], F32)
-        nc.gpsimd.tensor_scalar(gain[:], gn_t[:], 0.0625, 0.0, ALU.mult, ALU.add)
+        nc.scalar.activation(gain[:], gn_t[:], ACT.Copy, scale=0.0625)
+        w_deal = sb("w_deal", [P, PACK, P, 2], U8)
+        w_sc_deal = sb("w_sc_deal", [P, PACK, P], U8)
+        for t in range(PACK):
+            nc.gpsimd.tensor_copy(w_deal[:, t], w_w[:].rearrange("p (m t b) -> p t m b", t=PACK, b=2)[:, t])
+        nc.gpsimd.tensor_copy(w_sc_deal[:], w_sc[:].rearrange("p (m t) -> p t m", t=PACK))
+
+        key_sc_raw = sb("key_sc_raw", [P, S], U8)
+        key_sc = sb("stat_sc", [P, S], U8)
+        nc.vector.tensor_copy(key_sc_raw[:], d_sc[:].indirect(k1_t[:]))
+        nc.vector.tensor_copy(key_sc[:].rearrange("p (t m) -> p m t", t=PACK), key_sc_raw[:].rearrange("p (m t) -> p m t", t=PACK))
+        for r in range(1, 4):
+            nc.scalar.dma_start(key_sc[r:P:32, :].bitcast(I32), key_sc[8 * r : P : 32, :].bitcast(I32))
 
         two_sc = sb("two_sc", [P, S], U8)
         nc.vector.tensor_copy(two_sc[:], x_sc[:].indirect(two_t[:]))
         key_raw = sb("key_raw", [P, S], U32)
-        key_w = sb("key_w", [P, S], U32)
+        key_w = sb("stat_w", [P, S], U32)
         nc.vector.tensor_copy(key_raw[:], d_w[:].indirect(k1_t[:]))
         nc.vector.tensor_copy(
             key_w[:].bitcast(I32).rearrange("p (t m) -> p m t", t=PACK),
@@ -119,18 +125,11 @@ def tile_picked_twkssoftbwsum_none_po_kernel(
         nc.vector.tensor_copy(idx_sc[:], x_sc[:].indirect(offs_t[:]))
         nc.vector.tensor_copy(idx_w[:], x_w[:].indirect(offs_t[:]))
 
-        w_deal = sb("w_deal", [P, 2 * S], U8)
-        w_sc_deal = sb("w_sc_deal", [P, S], U8)
-        nc.vector.tensor_copy(
-            w_deal[:].rearrange("p (t m b) -> p m t b", t=PACK, b=2), w_w[:].rearrange("p (m t b) -> p m t b", t=PACK, b=2)
-        )
-        nc.vector.tensor_copy(w_sc_deal[:].rearrange("p (t m) -> p m t", t=PACK), w_sc[:].rearrange("p (m t) -> p m t", t=PACK))
-
         a_win = []
         for t in range(PACK):
             acc = scores(t, idx_w, idx_sc, f"bank{PACK + t}")
             a_win.append(sb(f"a_win{t}", [P, S], F32))
-            if t == 0:
+            if t < 1:
                 nc.scalar.activation(a_win[t][:], acc[:], ACT.Copy, scale=gain[:, t : t + 1])
             else:
                 nc.vector.tensor_scalar(a_win[t][:], acc[:], gain[:, t : t + 1], None, ALU.mult)
@@ -150,8 +149,8 @@ def tile_picked_twkssoftbwsum_none_po_kernel(
             nc.vector.quantize_mx(z_codes[:, lo:hi].bitcast(FP8X4), z_sc[:, lo:hi], z_bf[:])
             for t in range(PACK):
                 nc.tensor.matmul_mx(
-                    h_acc[t][:, lo:hi], lhsT=w_deal[:, 2 * t * P : 2 * (t + 1) * P].bitcast(FP4X4),
-                    lhsT_scale=w_sc_deal[:, t * P : (t + 1) * P],
+                    h_acc[t][:, lo:hi], lhsT=w_deal[:, t].rearrange("p m b -> p (m b)").bitcast(FP4X4),
+                    lhsT_scale=w_sc_deal[:, t],
                     rhs=z_codes[:, lo:hi].bitcast(FP8X4), rhs_scale=z_sc[:, lo:hi], start=True, stop=True,
                 )
 
@@ -161,35 +160,51 @@ def tile_picked_twkssoftbwsum_none_po_kernel(
             sig_h.append(sb(f"sig_h{t}", [P, S], F32))
             if t % 2 == 0:
                 nc.vector.tensor_copy(h_win[t][:], h_acc[t][:])
-            else:
+            elif t == 1:
                 nc.scalar.activation(h_win[t][:], h_acc[t][:], ACT.Copy)
 
         o_codes = sb("o_codes", [P, S], U32)
         o_sc = sb("o_sc", [P, S], U8)
         out_rows = out_0.rearrange("(p t) j -> p t j", t=PACK)
         out_words = out_1[0].rearrange("p n r -> p (n r)").bitcast(I32)
+        pending = []
         for lo, hi in O_PIECES:
             n = hi - lo
             gate = sb(f"gate{lo}", [P, PACK, n], F32)
             first = sb(f"first{lo}", [P, PACK, n], F32)
+            picked = sb(f"picked{lo}", [P, PACK, n], F32)
             second = sb(f"second{lo}", [P, PACK, n], F32)
             res = sb(f"res{lo}", [P, PACK, n], F32)
             for t in range(PACK):
                 if lo == 0:
+                    if t == 3:
+                        nc.scalar.activation(h_win[t][:], h_acc[t][:], ACT.Copy)
                     nc.scalar.activation(sig_h[t][:], h_win[t][:], ACT.Sigmoid)
                 nc.scalar.activation(gate[:, t, :], h_win[t][:].indirect(entries(n5_t, lo, hi)), ACT.Sigmoid)
-                nc.vector.tensor_tensor(first[:, t, :], h_win[t][:].indirect(entries(n3_t, lo, hi)), sig_h[t][:, lo:hi], ALU.mult)
-                nc.vector.tensor_tensor(second[:, t, :], h_win[t][:].indirect(entries(n4_t, lo, hi)), gate[:, t, :], ALU.mult)
+                if lo == 256:
+                    nc.scalar.activation(picked[:, t, :], h_win[t][:].indirect(entries(n3_t, lo, hi)), ACT.Copy)
+                    nc.vector.tensor_tensor(second[:, t, :], h_win[t][:].indirect(entries(n4_t, lo, hi)), gate[:, t, :], ALU.mult)
+                    nc.vector.tensor_tensor(first[:, t, :], picked[:, t, :], sig_h[t][:, lo:hi], ALU.mult)
+                else:
+                    nc.vector.tensor_tensor(first[:, t, :], h_win[t][:].indirect(entries(n3_t, lo, hi)), sig_h[t][:, lo:hi], ALU.mult)
+                    nc.vector.tensor_tensor(second[:, t, :], h_win[t][:].indirect(entries(n4_t, lo, hi)), gate[:, t, :], ALU.mult)
                 if t % 2 == 1:
                     nc.vector.tensor_tensor(res[:, t - 1 : t + 1, :], first[:, t - 1 : t + 1, :], second[:, t - 1 : t + 1, :], ALU.add)
+                if t == 1 and pending:
+                    pending.pop()()
             nc.sync.dma_start(out_rows[:, :, lo:hi], res[:])
-            o_bf = sb(f"o_bf{lo}", [P, PACK * n], BF16)
-            if hi < S:
-                nc.scalar.copy(woven(o_bf[:]), planes4(res[:]))
-            else:
-                nc.vector.tensor_copy(woven(o_bf[:]), planes4(res[:]))
-            nc.vector.quantize_mx(o_codes[:, lo:hi].bitcast(FP8X4), o_sc[:, lo:hi], o_bf[:])
-            nc.sync.dma_start(out_words[:, lo:hi], o_codes[:, lo:hi].bitcast(I32))
+
+            def planes(lo=lo, hi=hi, n=n, res=res):
+                o_bf = sb(f"o_bf{lo}", [P, PACK * n], BF16)
+                if hi < S:
+                    nc.scalar.copy(woven(o_bf[:]), planes4(res[:]))
+                else:
+                    nc.vector.tensor_copy(woven(o_bf[:]), planes4(res[:]))
+                nc.vector.quantize_mx(o_codes[:, lo:hi].bitcast(FP8X4), o_sc[:, lo:hi], o_bf[:])
+                nc.sync.dma_start(out_words[:, lo:hi], o_codes[:, lo:hi].bitcast(I32))
+
+            pending.append(planes)
+        pending.pop()()
         for q in range(4):
             eng = nc.sync if q % 2 else nc.scalar
             eng.dma_start(out_2[0].bitcast(I32)[4 * q : 4 * q + 4, :], o_sc[32 * q : 32 * q + 4, :].bitcast(I32))

@@ -16,8 +16,8 @@ PACK = 4
 TABLE = 2048
 S = 512
 FLOPS = 3 * 2 * 512 * 512 * 512
+HALVES = ((0, 256), (256, 512))
 Z_PIECES = ((0, 256), (256, 384), (384, 512))
-O_PIECES = ((0, 256), (256, 384), (384, 512))
 
 
 def tile_picked_twkssoftbwsum_none_po_kernel(
@@ -47,26 +47,26 @@ def tile_picked_twkssoftbwsum_none_po_kernel(
         d_sc = sb("d_sc", [P, TABLE], U8)
         x_sc = sb("x_sc", [P, TABLE], U8)
         w_sc = sb("w_sc", [P, S], U8)
+        nc.vector.memset(x_sc[:].bitcast(I32), 0)
         warm = sb("warm", [P, 1], F32)
         nc.vector.memset(warm[:], 0.0)
         warm_out = sb("warm_out", [P, 1], F32)
         nc.scalar.activation(warm_out[:], warm[:], ACT.Sigmoid)
 
-        nc.vector.memset(x_sc[:].bitcast(I32), 0)
         k1_t = load_list("k1_t", k1)
         nc.sync.dma_start(d_sc[:].bitcast(I32), d_scales[0].bitcast(I32).unsqueeze(1).to_broadcast([16, 8, TABLE // 4]))
         two_t = load_list("two_t", two)
         for q in range(4):
             nc.sync.dma_start(x_sc[32 * q : 32 * q + 4, :].bitcast(I32), x_scales[0].bitcast(I32)[4 * q : 4 * q + 4, :])
         d_w = sb("d_w", [P, TABLE], U32)
-        x_w = sb("x_w", [P, TABLE], U32)
         nc.sync.dma_start(d_w[:].bitcast(I32), d_words[0].rearrange("p n r -> p (n r)").bitcast(I32))
-        n2_t = load_list("n2_t", n2)
-        n1_t = load_list("n1_t", n1)
-        nc.sync.dma_start(x_w[:].bitcast(I32), x_words[0].rearrange("p n r -> p (n r)").bitcast(I32))
         offs_t = load_list("offs_t", offs)
-        n3_t = load_list("n3_t", n3)
+        n2_t = load_list("n2_t", n2)
+        x_w = sb("x_w", [P, TABLE], U32)
+        nc.sync.dma_start(x_w[:].bitcast(I32), x_words[0].rearrange("p n r -> p (n r)").bitcast(I32))
+        n1_t = load_list("n1_t", n1)
         n5_t = load_list("n5_t", n5)
+        n3_t = load_list("n3_t", n3)
         n4_t = load_list("n4_t", n4)
 
         w_w = sb("w_w", [P, 2 * S], U8)
@@ -112,12 +112,18 @@ def tile_picked_twkssoftbwsum_none_po_kernel(
             )
             return acc
 
+        def scaled_copy(win, acc, t):
+            if t % 2 == 0:
+                nc.scalar.activation(win[:], acc[:], ACT.Copy, scale=gain[:, t : t + 1])
+            else:
+                nc.vector.tensor_scalar(win[:], acc[:], gain[:, t : t + 1], None, ALU.mult)
+
         b_win, tanh_b = [], []
         for t in range(PACK):
             acc = scores(t, two_w, two_sc, f"bank{t}")
             b_win.append(sb(f"b_win{t}", [P, S], F32))
             tanh_b.append(sb(f"tanh_b{t}", [P, S], F32))
-            nc.scalar.activation(b_win[t][:], acc[:], ACT.Copy, scale=gain[:, t : t + 1])
+            scaled_copy(b_win[t], acc, t)
             nc.scalar.activation(tanh_b[t][:], acc[:], ACT.Tanh, scale=0.0625)
 
         idx_sc = sb("idx_sc", [P, S], U8)
@@ -129,82 +135,84 @@ def tile_picked_twkssoftbwsum_none_po_kernel(
         for t in range(PACK):
             acc = scores(t, idx_w, idx_sc, f"bank{PACK + t}")
             a_win.append(sb(f"a_win{t}", [P, S], F32))
-            if t < 1:
-                nc.scalar.activation(a_win[t][:], acc[:], ACT.Copy, scale=gain[:, t : t + 1])
-            else:
-                nc.vector.tensor_scalar(a_win[t][:], acc[:], gain[:, t : t + 1], None, ALU.mult)
+            scaled_copy(a_win[t], acc, t)
+
+        b_prod = sb("b_prod", [P, PACK, S], F32)
+        for lo, hi in HALVES:
+            for t in range(PACK):
+                nc.vector.tensor_tensor(b_prod[:, t, lo:hi], b_win[t][:].indirect(entries(n2_t, lo, hi)), tanh_b[t][:, lo:hi], ALU.mult)
 
         z_codes = sb("z_codes", [P, S], U32)
         z_sc = sb("z_sc", [P, S], U8)
-        h_acc = [psum.tile([P, S], F32, name=f"bank{t}") for t in range(PACK)]
+        h_acc = []
         for lo, hi in Z_PIECES:
             n = hi - lo
             a_pick = sb(f"a_pick{lo}", [P, PACK, n], F32)
-            b_prod = sb(f"b_prod{lo}", [P, PACK, n], F32)
             for t in range(PACK):
-                nc.vector.tensor_tensor(b_prod[:, t, :], b_win[t][:].indirect(entries(n2_t, lo, hi)), tanh_b[t][:, lo:hi], ALU.mult)
                 nc.scalar.activation(a_pick[:, t, :], a_win[t][:].indirect(entries(n1_t, lo, hi)), ACT.Copy)
-            z_bf = sb(f"z_bf{lo}", [P, PACK * n], BF16)
-            nc.vector.tensor_tensor(woven(z_bf[:]), planes4(a_pick[:]), planes4(b_prod[:]), ALU.subtract)
+            z_bf = sb("z_bf", [P, PACK * n], BF16)
+            nc.vector.tensor_tensor(woven(z_bf[:]), planes4(a_pick[:]), planes4(b_prod[:, :, lo:hi]), ALU.subtract)
             nc.vector.quantize_mx(z_codes[:, lo:hi].bitcast(FP8X4), z_sc[:, lo:hi], z_bf[:])
-            for t in range(PACK):
-                nc.tensor.matmul_mx(
-                    h_acc[t][:, lo:hi], lhsT=w_deal[:, t].rearrange("p m b -> p (m b)").bitcast(FP4X4),
-                    lhsT_scale=w_sc_deal[:, t],
-                    rhs=z_codes[:, lo:hi].bitcast(FP8X4), rhs_scale=z_sc[:, lo:hi], start=True, stop=True,
-                )
+            for u in range(2):
+                acc = psum.tile([P, 2, n], F32, name=f"bank{len(h_acc)}")
+                h_acc.append(acc)
+                for t in range(2 * u, 2 * u + 2):
+                    nc.tensor.matmul_mx(
+                        acc[:, t % 2, :], lhsT=w_deal[:, t].rearrange("p m b -> p (m b)").bitcast(FP4X4),
+                        lhsT_scale=w_sc_deal[:, t],
+                        rhs=z_codes[:, lo:hi].bitcast(FP8X4), rhs_scale=z_sc[:, lo:hi], start=True, stop=True,
+                    )
 
-        h_win, sig_h = [], []
-        for t in range(PACK):
-            h_win.append(sb(f"h_win{t}", [P, S], F32))
-            sig_h.append(sb(f"sig_h{t}", [P, S], F32))
-            if t % 2 == 0:
-                nc.vector.tensor_copy(h_win[t][:], h_acc[t][:])
-            elif t == 1:
-                nc.scalar.activation(h_win[t][:], h_acc[t][:], ACT.Copy)
+        h_win = [sb(f"h_win{t}", [P, S], F32) for t in range(PACK)]
+        sig_h = sb("sig_h", [P, PACK, S], F32)
+        for i, (lo, hi) in enumerate(Z_PIECES):
+            for t in range(PACK):
+                acc = h_acc[2 * i + t // 2]
+                if i == 0:
+                    nc.scalar.activation(h_win[t][:, lo:hi], acc[:, t % 2, :], ACT.Copy)
+                else:
+                    nc.vector.tensor_copy(h_win[t][:, lo:hi], acc[:, t % 2, :])
+            for u in range(2):
+                nc.scalar.activation(sig_h[:, 2 * u : 2 * u + 2, lo:hi], h_acc[2 * i + u][:], ACT.Sigmoid)
 
         o_codes = sb("o_codes", [P, S], U32)
         o_sc = sb("o_sc", [P, S], U8)
         out_rows = out_0.rearrange("(p t) j -> p t j", t=PACK)
         out_words = out_1[0].rearrange("p n r -> p (n r)").bitcast(I32)
-        pending = []
-        for lo, hi in O_PIECES:
-            n = hi - lo
-            gate = sb(f"gate{lo}", [P, PACK, n], F32)
-            first = sb(f"first{lo}", [P, PACK, n], F32)
-            picked = sb(f"picked{lo}", [P, PACK, n], F32)
-            second = sb(f"second{lo}", [P, PACK, n], F32)
-            res = sb(f"res{lo}", [P, PACK, n], F32)
+        n = S // 2
+        gate = sb("gate", [P, PACK, S], F32)
+        picked = sb("picked", [P, PACK, n], F32)
+        first = sb("first", [P, PACK, S], F32)
+        second = sb("second", [P, PACK, S], F32)
+        res = sb("res", [P, PACK, S], F32)
+        o_bf = sb("o_bf", [P, PACK * S], BF16)
+
+        def rounded(eng_copy, lo, hi):
+            eng_copy(woven(o_bf[:, PACK * lo : PACK * hi]), planes4(res[:, :, lo:hi]))
+
+        def planes(lo, hi):
+            nc.vector.quantize_mx(o_codes[:, lo:hi].bitcast(FP8X4), o_sc[:, lo:hi], o_bf[:, PACK * lo : PACK * hi])
+            nc.sync.dma_start(out_words[:, lo:hi], o_codes[:, lo:hi].bitcast(I32))
+
+        for lo, hi in HALVES:
             for t in range(PACK):
+                pair = slice(t - 1, t + 1)
+                nc.scalar.activation(gate[:, t, lo:hi], h_win[t][:].indirect(entries(n5_t, lo, hi)), ACT.Sigmoid)
                 if lo == 0:
-                    if t == 3:
-                        nc.scalar.activation(h_win[t][:], h_acc[t][:], ACT.Copy)
-                    nc.scalar.activation(sig_h[t][:], h_win[t][:], ACT.Sigmoid)
-                nc.scalar.activation(gate[:, t, :], h_win[t][:].indirect(entries(n5_t, lo, hi)), ACT.Sigmoid)
-                if lo == 256:
+                    nc.vector.tensor_tensor(first[:, t, lo:hi], h_win[t][:].indirect(entries(n3_t, lo, hi)), sig_h[:, t, lo:hi], ALU.mult)
+                else:
                     nc.scalar.activation(picked[:, t, :], h_win[t][:].indirect(entries(n3_t, lo, hi)), ACT.Copy)
-                    nc.vector.tensor_tensor(second[:, t, :], h_win[t][:].indirect(entries(n4_t, lo, hi)), gate[:, t, :], ALU.mult)
-                    nc.vector.tensor_tensor(first[:, t, :], picked[:, t, :], sig_h[t][:, lo:hi], ALU.mult)
-                else:
-                    nc.vector.tensor_tensor(first[:, t, :], h_win[t][:].indirect(entries(n3_t, lo, hi)), sig_h[t][:, lo:hi], ALU.mult)
-                    nc.vector.tensor_tensor(second[:, t, :], h_win[t][:].indirect(entries(n4_t, lo, hi)), gate[:, t, :], ALU.mult)
+                nc.vector.tensor_tensor(second[:, t, lo:hi], h_win[t][:].indirect(entries(n4_t, lo, hi)), gate[:, t, lo:hi], ALU.mult)
                 if t % 2 == 1:
-                    nc.vector.tensor_tensor(res[:, t - 1 : t + 1, :], first[:, t - 1 : t + 1, :], second[:, t - 1 : t + 1, :], ALU.add)
-                if t == 1 and pending:
-                    pending.pop()()
-            nc.sync.dma_start(out_rows[:, :, lo:hi], res[:])
-
-            def planes(lo=lo, hi=hi, n=n, res=res):
-                o_bf = sb(f"o_bf{lo}", [P, PACK * n], BF16)
-                if hi < S:
-                    nc.scalar.copy(woven(o_bf[:]), planes4(res[:]))
-                else:
-                    nc.vector.tensor_copy(woven(o_bf[:]), planes4(res[:]))
-                nc.vector.quantize_mx(o_codes[:, lo:hi].bitcast(FP8X4), o_sc[:, lo:hi], o_bf[:])
-                nc.sync.dma_start(out_words[:, lo:hi], o_codes[:, lo:hi].bitcast(I32))
-
-            pending.append(planes)
-        pending.pop()()
+                    if lo > 0:
+                        nc.vector.tensor_tensor(first[:, pair, lo:hi], picked[:, pair, :], sig_h[:, pair, lo:hi], ALU.mult)
+                    nc.vector.tensor_tensor(res[:, pair, lo:hi], first[:, pair, lo:hi], second[:, pair, lo:hi], ALU.add)
+                    nc.sync.dma_start(out_rows[:, pair, lo:hi], res[:, pair, lo:hi])
+        rounded(nc.scalar.copy, 0, n)
+        planes(0, n)
+        rounded(nc.scalar.copy, n, n + 96)
+        rounded(nc.vector.tensor_copy, n + 96, S)
+        planes(n, S)
         for q in range(4):
             eng = nc.sync if q % 2 else nc.scalar
             eng.dma_start(out_2[0].bitcast(I32)[4 * q : 4 * q + 4, :], o_sc[32 * q : 32 * q + 4, :].bitcast(I32))

import concourse.mybir as mybir

F32 = mybir.dt.float32
BF16 = mybir.dt.bfloat16
I32 = mybir.dt.int32
U32 = mybir.dt.uint32
U16 = mybir.dt.uint16
U8 = mybir.dt.uint8
FP8X4 = mybir.dt.float8_e4m3fn_x4
FP4X4 = mybir.dt.float4_e2m1fn_x4
ALU = mybir.AluOpType
ACT = mybir.ActivationFunctionType

P = 128
PACK = 4
TABLE = 2048
S = 512
FLOPS = 3 * 2 * 512 * 512 * 512
HALVES = ((0, 256), (256, 512))
Z_PIECES = ((0, 256), (256, 384), (384, 512))


def tile_picked_twkssoftbwsum_none_po_kernel(
    tc, x_words, x_scales, d_words, d_scales, gn, w1_words, w1_scales,
    offs, k1, two, n1, n2, n3, n4, n5, out_0, out_1, out_2,
):
    nc = tc.nc
    with tc.tile_pool(name="keep", bufs=1) as keep, tc.psum_pool(name="psum", bufs=1) as psum:

        def sb(name, shape, dtype):
            return keep.tile(shape, dtype, name=name, align_bytes=64)

        def load_list(name, src):
            t = sb(name, [P, S // 16], U16)
            nc.sync.dma_start(t[:], src)
            return t

        def entries(lst, lo, hi):
            return lst[:, lo // 16 : hi // 16]

        def woven(ap):
            return ap.rearrange("p (c i t) -> p c t i", i=4, t=PACK)

        def planes4(ap):
            return ap.rearrange("p t (c i) -> p c t i", i=4)

        d_sc = sb("d_sc", [P, TABLE], U8)
        x_sc = sb("x_sc", [P, TABLE], U8)
        w_sc = sb("w_sc", [P, S], U8)
        nc.vector.memset(x_sc[:].bitcast(I32), 0)
        warm = sb("warm", [P, 1], F32)
        nc.vector.memset(warm[:], 0.0)
        warm_out = sb("warm_out", [P, 1], F32)
        nc.scalar.activation(warm_out[:], warm[:], ACT.Sigmoid)

        k1_t = load_list("k1_t", k1)
        nc.sync.dma_start(d_sc[:].bitcast(I32), d_scales[0].bitcast(I32).unsqueeze(1).to_broadcast([16, 8, TABLE // 4]))
        two_t = load_list("two_t", two)
        for q in range(4):
            nc.sync.dma_start(x_sc[32 * q : 32 * q + 4, :].bitcast(I32), x_scales[0].bitcast(I32)[4 * q : 4 * q + 4, :])
        d_w = sb("d_w", [P, TABLE], U32)
        nc.sync.dma_start(d_w[:].bitcast(I32), d_words[0].rearrange("p n r -> p (n r)").bitcast(I32))
        offs_t = load_list("offs_t", offs)
        n2_t = load_list("n2_t", n2)
        x_w = sb("x_w", [P, TABLE], U32)
        nc.sync.dma_start(x_w[:].bitcast(I32), x_words[0].rearrange("p n r -> p (n r)").bitcast(I32))
        n1_t = load_list("n1_t", n1)
        n5_t = load_list("n5_t", n5)
        n3_t = load_list("n3_t", n3)
        n4_t = load_list("n4_t", n4)

        w_w = sb("w_w", [P, 2 * S], U8)
        nc.gpsimd.dma_start(w_w[:].bitcast(I32), w1_words[0].bitcast(I32))
        gn_t = sb("gn_t", [P, PACK], F32)
        nc.gpsimd.dma_start(gn_t[:], gn.rearrange("(p t) o -> p (t o)", t=PACK))
        nc.gpsimd.memset(w_sc[:].bitcast(I32), 0)
        for q in range(4):
            nc.gpsimd.dma_start(w_sc[32 * q : 32 * q + 4, :].bitcast(I32), w1_scales[0].bitcast(I32)[4 * q : 4 * q + 4, :])
        gain = sb("gain", [P, PACK], F32)
        nc.scalar.activation(gain[:], gn_t[:], ACT.Copy, scale=0.0625)
        w_deal = sb("w_deal", [P, PACK, P, 2], U8)
        w_sc_deal = sb("w_sc_deal", [P, PACK, P], U8)
        for t in range(PACK):
            nc.gpsimd.tensor_copy(w_deal[:, t], w_w[:].rearrange("p (m t b) -> p t m b", t=PACK, b=2)[:, t])
        nc.gpsimd.tensor_copy(w_sc_deal[:], w_sc[:].rearrange("p (m t) -> p t m", t=PACK))

        key_sc_raw = sb("key_sc_raw", [P, S], U8)
        key_sc = sb("stat_sc", [P, S], U8)
        nc.vector.tensor_copy(key_sc_raw[:], d_sc[:].indirect(k1_t[:]))
        nc.vector.tensor_copy(key_sc[:].rearrange("p (t m) -> p m t", t=PACK), key_sc_raw[:].rearrange("p (m t) -> p m t", t=PACK))
        for r in range(1, 4):
            nc.scalar.dma_start(key_sc[r:P:32, :].bitcast(I32), key_sc[8 * r : P : 32, :].bitcast(I32))

        two_sc = sb("two_sc", [P, S], U8)
        nc.vector.tensor_copy(two_sc[:], x_sc[:].indirect(two_t[:]))
        key_raw = sb("key_raw", [P, S], U32)
        key_w = sb("stat_w", [P, S], U32)
        nc.vector.tensor_copy(key_raw[:], d_w[:].indirect(k1_t[:]))
        nc.vector.tensor_copy(
            key_w[:].bitcast(I32).rearrange("p (t m) -> p m t", t=PACK),
            key_raw[:].bitcast(I32).rearrange("p (m t) -> p m t", t=PACK),
        )
        two_w = sb("two_w", [P, S], U32)
        nc.vector.tensor_copy(two_w[:], x_w[:].indirect(two_t[:]))

        def scores(t, words, scales, tag):
            acc = psum.tile([P, S], F32, name=tag)
            cols = slice(t * P, (t + 1) * P)
            nc.tensor.matmul_mx(
                acc[:], lhsT=key_w[:, cols].bitcast(FP8X4), lhsT_scale=key_sc[:, cols],
                rhs=words[:].bitcast(FP8X4), rhs_scale=scales[:], start=True, stop=True,
            )
            return acc

        def scaled_copy(win, acc, t):
            if t % 2 == 0:
                nc.scalar.activation(win[:], acc[:], ACT.Copy, scale=gain[:, t : t + 1])
            else:
                nc.vector.tensor_scalar(win[:], acc[:], gain[:, t : t + 1], None, ALU.mult)

        b_win, tanh_b = [], []
        for t in range(PACK):
            acc = scores(t, two_w, two_sc, f"bank{t}")
            b_win.append(sb(f"b_win{t}", [P, S], F32))
            tanh_b.append(sb(f"tanh_b{t}", [P, S], F32))
            scaled_copy(b_win[t], acc, t)
            nc.scalar.activation(tanh_b[t][:], acc[:], ACT.Tanh, scale=0.0625)

        idx_sc = sb("idx_sc", [P, S], U8)
        idx_w = sb("idx_w", [P, S], U32)
        nc.vector.tensor_copy(idx_sc[:], x_sc[:].indirect(offs_t[:]))
        nc.vector.tensor_copy(idx_w[:], x_w[:].indirect(offs_t[:]))

        a_win = []
        for t in range(PACK):
            acc = scores(t, idx_w, idx_sc, f"bank{PACK + t}")
            a_win.append(sb(f"a_win{t}", [P, S], F32))
            scaled_copy(a_win[t], acc, t)

        b_prod = sb("b_prod", [P, PACK, S], F32)
        for lo, hi in HALVES:
            for t in range(PACK):
                nc.vector.tensor_tensor(b_prod[:, t, lo:hi], b_win[t][:].indirect(entries(n2_t, lo, hi)), tanh_b[t][:, lo:hi], ALU.mult)

        z_codes = sb("z_codes", [P, S], U32)
        z_sc = sb("z_sc", [P, S], U8)
        h_acc = []
        for lo, hi in Z_PIECES:
            n = hi - lo
            a_pick = sb(f"a_pick{lo}", [P, PACK, n], F32)
            for t in range(PACK):
                nc.scalar.activation(a_pick[:, t, :], a_win[t][:].indirect(entries(n1_t, lo, hi)), ACT.Copy)
            z_bf = sb("z_bf", [P, PACK * n], BF16)
            nc.vector.tensor_tensor(woven(z_bf[:]), planes4(a_pick[:]), planes4(b_prod[:, :, lo:hi]), ALU.subtract)
            nc.vector.quantize_mx(z_codes[:, lo:hi].bitcast(FP8X4), z_sc[:, lo:hi], z_bf[:])
            for u in range(2):
                acc = psum.tile([P, 2, n], F32, name=f"bank{len(h_acc)}")
                h_acc.append(acc)
                for t in range(2 * u, 2 * u + 2):
                    nc.tensor.matmul_mx(
                        acc[:, t % 2, :], lhsT=w_deal[:, t].rearrange("p m b -> p (m b)").bitcast(FP4X4),
                        lhsT_scale=w_sc_deal[:, t],
                        rhs=z_codes[:, lo:hi].bitcast(FP8X4), rhs_scale=z_sc[:, lo:hi], start=True, stop=True,
                    )

        h_win = [sb(f"h_win{t}", [P, S], F32) for t in range(PACK)]
        sig_h = sb("sig_h", [P, PACK, S], F32)
        for i, (lo, hi) in enumerate(Z_PIECES):
            for t in range(PACK):
                acc = h_acc[2 * i + t // 2]
                if i == 0:
                    nc.scalar.activation(h_win[t][:, lo:hi], acc[:, t % 2, :], ACT.Copy)
                else:
                    nc.vector.tensor_copy(h_win[t][:, lo:hi], acc[:, t % 2, :])
            for u in range(2):
                nc.scalar.activation(sig_h[:, 2 * u : 2 * u + 2, lo:hi], h_acc[2 * i + u][:], ACT.Sigmoid)

        o_codes = sb("o_codes", [P, S], U32)
        o_sc = sb("o_sc", [P, S], U8)
        out_rows = out_0.rearrange("(p t) j -> p t j", t=PACK)
        out_words = out_1[0].rearrange("p n r -> p (n r)").bitcast(I32)
        n = S // 2
        gate = sb("gate", [P, PACK, S], F32)
        picked = sb("picked", [P, PACK, n], F32)
        first = sb("first", [P, PACK, S], F32)
        second = sb("second", [P, PACK, S], F32)
        res = sb("res", [P, PACK, S], F32)
        o_bf = sb("o_bf", [P, PACK * S], BF16)

        def rounded(eng_copy, lo, hi):
            eng_copy(woven(o_bf[:, PACK * lo : PACK * hi]), planes4(res[:, :, lo:hi]))

        def planes(lo, hi):
            nc.vector.quantize_mx(o_codes[:, lo:hi].bitcast(FP8X4), o_sc[:, lo:hi], o_bf[:, PACK * lo : PACK * hi])
            nc.sync.dma_start(out_words[:, lo:hi], o_codes[:, lo:hi].bitcast(I32))

        for lo, hi in HALVES:
            for t in range(PACK):
                pair = slice(t - 1, t + 1)
                nc.scalar.activation(gate[:, t, lo:hi], h_win[t][:].indirect(entries(n5_t, lo, hi)), ACT.Sigmoid)
                if lo == 0:
                    nc.vector.tensor_tensor(first[:, t, lo:hi], h_win[t][:].indirect(entries(n3_t, lo, hi)), sig_h[:, t, lo:hi], ALU.mult)
                else:
                    nc.scalar.activation(picked[:, t, :], h_win[t][:].indirect(entries(n3_t, lo, hi)), ACT.Copy)
                nc.vector.tensor_tensor(second[:, t, lo:hi], h_win[t][:].indirect(entries(n4_t, lo, hi)), gate[:, t, lo:hi], ALU.mult)
                if t % 2 == 1:
                    if lo > 0:
                        nc.vector.tensor_tensor(first[:, pair, lo:hi], picked[:, pair, :], sig_h[:, pair, lo:hi], ALU.mult)
                    nc.vector.tensor_tensor(res[:, pair, lo:hi], first[:, pair, lo:hi], second[:, pair, lo:hi], ALU.add)
                    nc.sync.dma_start(out_rows[:, pair, lo:hi], res[:, pair, lo:hi])
        rounded(nc.scalar.copy, 0, n)
        planes(0, n)
        rounded(nc.scalar.copy, n, n + 96)
        rounded(nc.vector.tensor_copy, n + 96, S)
        planes(n, S)
        for q in range(4):
            eng = nc.sync if q % 2 else nc.scalar
            eng.dma_start(out_2[0].bitcast(I32)[4 * q : 4 * q + 4, :], o_sc[32 * q : 32 * q + 4, :].bitcast(I32))
